import numpy as np, ml_dtypes
CORES = [9,17,57,81,121,137,145,185,209,249]
N = 10
import mx_ref
NC, WT = 256, 1
BF = ml_dtypes.bfloat16
def pk(c, s, i=0):
    return (np.ascontiguousarray(c[:, 512 * i:512 * i + 512]), mx_ref.live(s[:, 128 * i:128 * i + 128]))
def inputs(rng, e, E):
    def f(*shape):
        v = (rng.standard_normal(shape, dtype=np.float32) * np.exp2(rng.integers(-2, 3, shape[:-1] + (1,)))).astype(BF)
        return mx_ref.spread((v.astype(np.float32) * np.exp2(rng.integers(-E, E + 1, shape[:-2] + (1, 1))).astype(np.float32)).astype(BF), rng, e)
    def packed(k):
        c = np.zeros((N, 128, k * 512), np.uint8); s = np.zeros((N, 128, k * 128), np.uint8)
        for r in range(N):
            for i in range(k):
                a, b = mx_ref.quantize(f(128, 512)); c[r][:, 512 * i:512 * i + 512] = a; s[r][:, 128 * i:128 * i + 128] = mx_ref.plane(b, rng)
        return c, s
    d = {}
    d["wc"], d["ws"] = packed(WT)
    d["x"] = f(N, 128, 4 * NC)
    return d
def setup_inputs(rng):
    return inputs(rng, 0, 0)
def setup_inputs_blocks(rng):
    return inputs(rng, 4, 0)
def setup_inputs_wide(rng):
    return inputs(rng, 0, 8)
def reference(wc, ws, x):
    y = np.zeros((N, 128, N * WT * NC), np.float32)
    for r in range(N):
        X = mx_ref.quantize(x[r])
        for b in range(N * WT):
            y[r][:, NC * b:NC * b + NC] = mx_ref.matmul(pk(wc[b // WT], ws[b // WT], b % WT), X)
    return {"y": y}

@@ -1,0 +1,150 @@
+from concourse.bass import DstId, RemoteDMATransfer
+from concourse.mybir import dt, ActivationFunctionType
+
+N = 10
+WORLD = 256
+WW = 128
+NC = 256
+BANK = 512
+BANKS = 8
+DIRECT = 3
+
+SCRATCH = {
+    "wcd": ("dram", [128, WW], "float8_e4m3fn_x4"),
+    "wsd": ("dram", [128, WW], "uint8"),
+    "wq": ("sbuf", [128, N * WW], "float8_e4m3fn_x4"),
+    "wp": ("sbuf", [128, N * WW], "uint8"),
+    "xb": ("sbuf", [128, 4 * NC], "bfloat16"),
+    "xq": ("sbuf", [128, NC], "float8_e4m3fn_x4"),
+    "xs": ("sbuf", [128, NC], "uint8"),
+    "yb": ("sbuf", [128, N * NC], "float32"),
+    "ps": ("psum", [128, BANKS * BANK], "float32"),
+}
+SEMAPHORES = (["ls", "lc", "lo", "lx", "qx", "hs", "hc", "sent", "st"]
+              + ["arr%d" % j for j in range(N)] + ["mm%d" % k for k in range(N)] + ["cp%d" % k for k in range(N)])
+
+
+def bits(m):
+    return bin(m).count("1")
+
+
+def plan(cores, topo):
+    hand, jobs, due = {}, {}, {}
+    for j, s in enumerate(cores):
+        mine = [t for t in cores if t == s or topo.same_plane(s, t)]
+        far = [t for t in cores if t not in mine]
+        i, m = mine.index(s), len(far)
+        ring = [mine[(i + k) % len(mine)] for k in range(1, len(mine))]
+        cross = [far[(i + k) % m] for k in range(m)]
+        chipm = [c for c in range(WORLD) if c != s and topo.host(c) == topo.host(s) and topo.chip(c) == topo.chip(s)]
+        ports = [c for c in chipm if topo.may_write(c, far[0])]
+        near = [c for c in ports if topo.die(c) == topo.die(s)]
+        off = [c for c in ports if topo.die(c) != topo.die(s)]
+        plain = [c for c in chipm if c not in ports and topo.die(c) != topo.die(s)]
+        a, b, c2, d = near[0], off[0], off[1], plain[0]
+        ks = {a: [k for k in range(m) if k % 3 == 0][:m // 3]}
+        rest = [k for k in range(m) if k not in ks[a]]
+        ks[b], ks[c2] = rest[0::2], rest[1::2]
+        lists = {h: [cross[k] for k in sorted(ks[h], key=lambda k: (k % 2, k))] for h in (a, b, c2)}
+        lists[d] = []
+        for t in ring[DIRECT:]:
+            lists[min((b, c2, d), key=lambda h: len(lists[h]))].append(t)
+        hand[s] = [h for h in (a, b, c2, d) if lists[h]]
+        jobs[s] = (j, ring[:DIRECT])
+        for p, t in enumerate(ring[:DIRECT]):
+            due[(j, t)] = (1, p)
+        for h in hand[s]:
+            jobs[h] = (j, lists[h])
+            for p, t in enumerate(lists[h]):
+                due[(j, t)] = (2, p)
+    return hand, jobs, due
+
+
+def engines(core, dsts, topo):
+    m = topo.mask(core, dsts[0])
+    for t in dsts[1:]:
+        m &= topo.mask(core, t)
+    return m
+
+
+def rank_program(g, core, T, topo):
+    cores = list(T.cores)
+    hand, jobs, due = plan(cores, topo)
+    if core not in jobs:
+        return
+    tile, dsts = jobs[core]
+    rank = T.rank_of(core)
+    helpers = hand[core] if rank is not None else []
+    mask = engines(core, dsts + helpers, topo)
+    ne = bits(mask)
+    sent = [0]
+
+    def write(to, src, dst, sem):
+        ids = []
+        for t in to:
+            rid, pid = topo.addr(t, core)
+            ids.append(DstId(rid=rid, pnc=pid))
+        g.remote_dma_fused([RemoteDMATransfer(dst_ids=ids, dma_engine_mask=mask, remote_sem=sem, srcs=[src],
+                                              dsts=[dst for _ in to])], local_sem=T.sem.sent)
+        sent[0] += ne
+
+    lo, hi = tile * WW, (tile + 1) * WW
+    arr = T.sem["arr%d" % tile]
+    codes_d, plane_d = T.wcd[:].bitcast(dt.uint8), T.wsd[:]
+    codes_s, plane_s = T.wq[:, lo:hi].bitcast(dt.uint8), T.wp[:, lo:hi]
+
+    if rank is None:
+        g.wait_ge(T.sem.hs, bits(engines(cores[tile], jobs[cores[tile]][1] + hand[cores[tile]], topo)))
+        write(dsts, plane_d, plane_s, arr)
+        g.wait_ge(T.sem.hc, bits(engines(cores[tile], jobs[cores[tile]][1] + hand[cores[tile]], topo)))
+        for t in dsts:
+            write([t], codes_d, codes_s, arr)
+        g.wait_ge(T.sem.sent, sent[0])
+        return
+
+    g.scalar.dma_start(plane_d, T.ws[:]).then_inc(T.sem.ls, 16)
+    g.sync.dma_start(codes_d, T.wc[:]).then_inc(T.sem.lc, 16)
+    g.sync.dma_start(T.xb[:], T.x[:]).then_inc(T.sem.lx, 16)
+    g.scalar.dma_start(plane_s, T.ws[:]).then_inc(T.sem.lo, 16)
+    g.scalar.dma_start(codes_s, T.wc[:]).then_inc(T.sem.lo, 16)
+
+    g.wait_ge(T.sem.ls, 16)
+    write(helpers, plane_d, plane_d, T.sem.hs)
+    g.wait_ge(T.sem.lc, 16)
+    write(helpers, codes_d, codes_d, T.sem.hc)
+    write(dsts, plane_d, plane_s, arr)
+    for t in dsts:
+        write([t], codes_d, codes_s, arr)
+
+    g.vector.wait_ge(T.sem.lx, 16)
+    g.vector.quantize_mx(T.xq[:], T.xs[:], T.xb[:]).then_inc(T.sem.qx, 1)
+    sender = {}
+    for c, (j, l) in jobs.items():
+        for t in l:
+            sender[(j, t)] = c
+    order = [rank] + sorted((j for j in range(N) if j != rank), key=lambda j: (due[(j, core)], j))
+    g.tensor.wait_ge(T.sem.qx, 1)
+    g.tensor.wait_ge(T.sem.lo, 32)
+    for k, j in enumerate(order):
+        if j != rank:
+            c = sender[(j, core)]
+            g.tensor.wait_ge(T.sem["arr%d" % j], 2 * bits(engines(c, jobs[c][1] + (hand[c] if c in hand else []), topo)))
+        if k >= BANKS:
+            g.tensor.wait_ge(T.sem["cp%d" % (k - BANKS)], 1)
+        bank = T.ps[:, (k % BANKS) * BANK:(k % BANKS) * BANK + NC]
+        g.tensor.matmul_mx(bank, T.wq[:, j * WW:(j + 1) * WW], T.wp[:, j * WW:(j + 1) * WW], T.xq[:], T.xs[:],
+                           True, True).then_inc(T.sem["mm%d" % k], 1)
+        blk = T.yb[:, j * NC:(j + 1) * NC]
+        if k % 2 == 0:
+            g.vector.wait_ge(T.sem["mm%d" % k], 1)
+            g.vector.tensor_copy(blk, bank).then_inc(T.sem["cp%d" % k], 1)
+            q = g.sync
+        else:
+            g.scalar.wait_ge(T.sem["mm%d" % k], 1)
+            g.scalar.activation(blk, bank, ActivationFunctionType.Copy).then_inc(T.sem["cp%d" % k], 1)
+            q = g.scalar
+        q.wait_ge(T.sem["cp%d" % k], 1)
+        q.dma_start(T.y[:, j * NC:(j + 1) * NC], blk).then_inc(T.sem.st, 16)
+
+    g.wait_ge(T.sem.sent, sent[0])
+    g.wait_ge(T.sem.st, 16 * N)

@@ -20,7 +20,7 @@ SCRATCH = {
     "yb": ("sbuf", [128, N * NC], "float32"),
     "ps": ("psum", [128, BANKS * BANK], "float32"),
 }
-SEMAPHORES = (["ls", "lc", "lo", "lx", "qx", "hs", "hc", "sent", "st"]
+SEMAPHORES = (["ls", "lc", "lo", "lx", "qx", "hs", "hc", "sent", "st", "mmx"]
               + ["arr%d" % j for j in range(N)] + ["mm%d" % k for k in range(N)] + ["cp%d" % k for k in range(N)])
 
 
@@ -28,8 +28,32 @@ def bits(m):
     return bin(m).count("1")
 
 
+def slots_of(cores, fw, k):
+    left = {s: list(fw[s]) for s in cores}
+    out = []
+    for _ in range(k):
+        match = {}
+
+        def seat(s, seen):
+            for t in left[s]:
+                if t not in seen:
+                    seen.add(t)
+                    if t not in match or seat(match[t], seen):
+                        match[t] = s
+                        return True
+            return False
+
+        for s in cores:
+            seat(s, set())
+        slot = {s: t for t, s in match.items()}
+        for s in cores:
+            left[s].remove(slot[s])
+        out.append(slot)
+    return out
+
+
 def plan(cores, topo):
-    hand, jobs, due = {}, {}, {}
+    hand, jobs, due, fw = {}, {}, {}, {}
     for j, s in enumerate(cores):
         mine = [t for t in cores if t == s or topo.same_plane(s, t)]
         far = [t for t in cores if t not in mine]
@@ -40,23 +64,19 @@ def plan(cores, topo):
         ports = [c for c in chipm if topo.may_write(c, far[0])]
         near = [c for c in ports if topo.die(c) == topo.die(s)]
         off = [c for c in ports if topo.die(c) != topo.die(s)]
-        plain = [c for c in chipm if c not in ports and topo.die(c) != topo.die(s)]
-        a, b, c2, d = near[0], off[0], off[1], plain[0]
-        ks = {a: [k for k in range(m) if k % 3 == 0][:m // 3]}
-        rest = [k for k in range(m) if k not in ks[a]]
-        ks[b], ks[c2] = rest[0::2], rest[1::2]
-        lists = {h: [cross[k] for k in sorted(ks[h], key=lambda k: (k % 2, k))] for h in (a, b, c2)}
-        lists[d] = []
-        for t in ring[DIRECT:]:
-            lists[min((b, c2, d), key=lambda h: len(lists[h]))].append(t)
-        hand[s] = [h for h in (a, b, c2, d) if lists[h]]
+        hand[s] = [off[0], off[1], near[0]]
+        fw[s] = cross + ring[DIRECT:]
         jobs[s] = (j, ring[:DIRECT])
         for p, t in enumerate(ring[:DIRECT]):
-            due[(j, t)] = (1, p)
-        for h in hand[s]:
-            jobs[h] = (j, lists[h])
-            for p, t in enumerate(lists[h]):
-                due[(j, t)] = (2, p)
+            due[(j, t)] = (1, p, 0)
+    nh = len(hand[cores[0]])
+    sl = slots_of(cores, fw, 2 * nh)
+    for j, s in enumerate(cores):
+        for n, h in enumerate(hand[s]):
+            l = [sl[n][s], sl[nh + n][s]]
+            jobs[h] = (j, l)
+            for p, t in enumerate(l):
+                due[(j, t)] = (2, p, n)
     return hand, jobs, due
 
 
@@ -74,19 +94,20 @@ def rank_program(g, core, T, topo):
         return
     tile, dsts = jobs[core]
     rank = T.rank_of(core)
-    helpers = hand[core] if rank is not None else []
-    mask = engines(core, dsts + helpers, topo)
-    ne = bits(mask)
+    owner = cores[tile]
+    out = engines(core, dsts, topo)
+    h_codes = engines(owner, hand[owner], topo)
+    h_plane = h_codes & engines(owner, jobs[owner][1], topo)
     sent = [0]
 
-    def write(to, src, dst, sem):
+    def write(to, src, dst, sem, mask):
         ids = []
         for t in to:
             rid, pid = topo.addr(t, core)
             ids.append(DstId(rid=rid, pnc=pid))
         g.remote_dma_fused([RemoteDMATransfer(dst_ids=ids, dma_engine_mask=mask, remote_sem=sem, srcs=[src],
                                               dsts=[dst for _ in to])], local_sem=T.sem.sent)
-        sent[0] += ne
+        sent[0] += bits(mask)
 
     lo, hi = tile * WW, (tile + 1) * WW
     arr = T.sem["arr%d" % tile]
@@ -94,11 +115,10 @@ def rank_program(g, core, T, topo):
     codes_s, plane_s = T.wq[:, lo:hi].bitcast(dt.uint8), T.wp[:, lo:hi]
 
     if rank is None:
-        g.wait_ge(T.sem.hs, bits(engines(cores[tile], jobs[cores[tile]][1] + hand[cores[tile]], topo)))
-        write(dsts, plane_d, plane_s, arr)
-        g.wait_ge(T.sem.hc, bits(engines(cores[tile], jobs[cores[tile]][1] + hand[cores[tile]], topo)))
-        for t in dsts:
-            write([t], codes_d, codes_s, arr)
+        g.wait_ge(T.sem.hs, bits(h_plane))
+        write(dsts, plane_d, plane_s, arr, out)
+        g.wait_ge(T.sem.hc, bits(h_codes))
+        write(dsts, codes_d, codes_s, arr, out)
         g.wait_ge(T.sem.sent, sent[0])
         return
 
@@ -109,12 +129,11 @@ def rank_program(g, core, T, topo):
     g.scalar.dma_start(codes_s, T.wc[:]).then_inc(T.sem.lo, 16)
 
     g.wait_ge(T.sem.ls, 16)
-    write(helpers, plane_d, plane_d, T.sem.hs)
+    write(hand[core], plane_d, plane_d, T.sem.hs, h_plane)
     g.wait_ge(T.sem.lc, 16)
-    write(helpers, codes_d, codes_d, T.sem.hc)
-    write(dsts, plane_d, plane_s, arr)
-    for t in dsts:
-        write([t], codes_d, codes_s, arr)
+    write(hand[core], codes_d, codes_d, T.sem.hc, h_codes)
+    write(dsts, plane_d, plane_s, arr, out)
+    write(dsts, codes_d, codes_s, arr, out)
 
     g.vector.wait_ge(T.sem.lx, 16)
     g.vector.quantize_mx(T.xq[:], T.xs[:], T.xb[:]).then_inc(T.sem.qx, 1)
@@ -126,24 +145,39 @@ def rank_program(g, core, T, topo):
     g.tensor.wait_ge(T.sem.qx, 1)
     g.tensor.wait_ge(T.sem.lo, 32)
     for k, j in enumerate(order):
+        w, wpl = T.wq[:, j * WW:(j + 1) * WW], T.wp[:, j * WW:(j + 1) * WW]
+        blk = T.yb[:, j * NC:(j + 1) * NC]
+        mm, cp = T.sem["mm%d" % k], T.sem["cp%d" % k]
         if j != rank:
             c = sender[(j, core)]
-            g.tensor.wait_ge(T.sem["arr%d" % j], 2 * bits(engines(c, jobs[c][1] + (hand[c] if c in hand else []), topo)))
+            g.tensor.wait_ge(T.sem["arr%d" % j], 2 * bits(engines(c, jobs[c][1], topo)))
         if k >= BANKS:
             g.tensor.wait_ge(T.sem["cp%d" % (k - BANKS)], 1)
-        bank = T.ps[:, (k % BANKS) * BANK:(k % BANKS) * BANK + NC]
-        g.tensor.matmul_mx(bank, T.wq[:, j * WW:(j + 1) * WW], T.wp[:, j * WW:(j + 1) * WW], T.xq[:], T.xs[:],
-                           True, True).then_inc(T.sem["mm%d" % k], 1)
-        blk = T.yb[:, j * NC:(j + 1) * NC]
-        if k % 2 == 0:
-            g.vector.wait_ge(T.sem["mm%d" % k], 1)
-            g.vector.tensor_copy(blk, bank).then_inc(T.sem["cp%d" % k], 1)
+        b0 = (k % BANKS) * BANK
+        if k == N - 1:
+            h = NC // 2
+            b1 = ((k + 1) % BANKS) * BANK
+            g.tensor.wait_ge(T.sem["cp%d" % (k + 1 - BANKS)], 1)
+            g.tensor.matmul_mx(T.ps[:, b0:b0 + h], w, wpl, T.xq[:, 0:h], T.xs[:, 0:h], True, True).then_inc(mm, 1)
+            g.tensor.matmul_mx(T.ps[:, b1:b1 + h], w, wpl, T.xq[:, h:NC], T.xs[:, h:NC], True, True).then_inc(T.sem.mmx, 1)
+            g.vector.wait_ge(mm, 1)
+            g.vector.tensor_copy(T.yb[:, j * NC:j * NC + h], T.ps[:, b0:b0 + h]).then_inc(cp, 1)
+            g.vector.wait_ge(T.sem.mmx, 1)
+            g.vector.tensor_copy(T.yb[:, j * NC + h:(j + 1) * NC], T.ps[:, b1:b1 + h]).then_inc(cp, 1)
+            g.sync.wait_ge(cp, 2)
+            g.sync.dma_start(T.y[:, j * NC:(j + 1) * NC], blk).then_inc(T.sem.st, 16)
+            continue
+        bank = T.ps[:, b0:b0 + NC]
+        g.tensor.matmul_mx(bank, w, wpl, T.xq[:], T.xs[:], True, True).then_inc(mm, 1)
+        if (N - 1 - k) % 2 == 0:
+            g.vector.wait_ge(mm, 1)
+            g.vector.tensor_copy(blk, bank).then_inc(cp, 1)
             q = g.sync
         else:
-            g.scalar.wait_ge(T.sem["mm%d" % k], 1)
-            g.scalar.activation(blk, bank, ActivationFunctionType.Copy).then_inc(T.sem["cp%d" % k], 1)
+            g.scalar.wait_ge(mm, 1)
+            g.scalar.activation(blk, bank, ActivationFunctionType.Copy).then_inc(cp, 1)
             q = g.scalar
-        q.wait_ge(T.sem["cp%d" % k], 1)
+        q.wait_ge(cp, 1)
         q.dma_start(T.y[:, j * NC:(j + 1) * NC], blk).then_inc(T.sem.st, 16)
 
     g.wait_ge(T.sem.sent, sent[0])

from concourse.bass import DstId, RemoteDMATransfer
from concourse.mybir import dt, ActivationFunctionType

N = 10
WORLD = 256
WW = 128
NC = 256
BANK = 512
BANKS = 8
DIRECT = 3

SCRATCH = {
    "wcd": ("dram", [128, WW], "float8_e4m3fn_x4"),
    "wsd": ("dram", [128, WW], "uint8"),
    "wq": ("sbuf", [128, N * WW], "float8_e4m3fn_x4"),
    "wp": ("sbuf", [128, N * WW], "uint8"),
    "xb": ("sbuf", [128, 4 * NC], "bfloat16"),
    "xq": ("sbuf", [128, NC], "float8_e4m3fn_x4"),
    "xs": ("sbuf", [128, NC], "uint8"),
    "yb": ("sbuf", [128, N * NC], "float32"),
    "ps": ("psum", [128, BANKS * BANK], "float32"),
}
SEMAPHORES = (["ls", "lc", "lo", "lx", "qx", "hs", "hc", "sent", "st", "mmx"]
              + ["arr%d" % j for j in range(N)] + ["mm%d" % k for k in range(N)] + ["cp%d" % k for k in range(N)])


def bits(m):
    return bin(m).count("1")


def slots_of(cores, fw, k):
    left = {s: list(fw[s]) for s in cores}
    out = []
    for _ in range(k):
        match = {}

        def seat(s, seen):
            for t in left[s]:
                if t not in seen:
                    seen.add(t)
                    if t not in match or seat(match[t], seen):
                        match[t] = s
                        return True
            return False

        for s in cores:
            seat(s, set())
        slot = {s: t for t, s in match.items()}
        for s in cores:
            left[s].remove(slot[s])
        out.append(slot)
    return out


def plan(cores, topo):
    hand, jobs, due, fw = {}, {}, {}, {}
    for j, s in enumerate(cores):
        mine = [t for t in cores if t == s or topo.same_plane(s, t)]
        far = [t for t in cores if t not in mine]
        i, m = mine.index(s), len(far)
        ring = [mine[(i + k) % len(mine)] for k in range(1, len(mine))]
        cross = [far[(i + k) % m] for k in range(m)]
        chipm = [c for c in range(WORLD) if c != s and topo.host(c) == topo.host(s) and topo.chip(c) == topo.chip(s)]
        ports = [c for c in chipm if topo.may_write(c, far[0])]
        near = [c for c in ports if topo.die(c) == topo.die(s)]
        off = [c for c in ports if topo.die(c) != topo.die(s)]
        hand[s] = [off[0], off[1], near[0]]
        fw[s] = cross + ring[DIRECT:]
        jobs[s] = (j, ring[:DIRECT])
        for p, t in enumerate(ring[:DIRECT]):
            due[(j, t)] = (1, p, 0)
    nh = len(hand[cores[0]])
    sl = slots_of(cores, fw, 2 * nh)
    for j, s in enumerate(cores):
        for n, h in enumerate(hand[s]):
            l = [sl[n][s], sl[nh + n][s]]
            jobs[h] = (j, l)
            for p, t in enumerate(l):
                due[(j, t)] = (2, p, n)
    return hand, jobs, due


def engines(core, dsts, topo):
    m = topo.mask(core, dsts[0])
    for t in dsts[1:]:
        m &= topo.mask(core, t)
    return m


def rank_program(g, core, T, topo):
    cores = list(T.cores)
    hand, jobs, due = plan(cores, topo)
    if core not in jobs:
        return
    tile, dsts = jobs[core]
    rank = T.rank_of(core)
    owner = cores[tile]
    out = engines(core, dsts, topo)
    h_codes = engines(owner, hand[owner], topo)
    h_plane = h_codes & engines(owner, jobs[owner][1], topo)
    sent = [0]

    def write(to, src, dst, sem, mask):
        ids = []
        for t in to:
            rid, pid = topo.addr(t, core)
            ids.append(DstId(rid=rid, pnc=pid))
        g.remote_dma_fused([RemoteDMATransfer(dst_ids=ids, dma_engine_mask=mask, remote_sem=sem, srcs=[src],
                                              dsts=[dst for _ in to])], local_sem=T.sem.sent)
        sent[0] += bits(mask)

    lo, hi = tile * WW, (tile + 1) * WW
    arr = T.sem["arr%d" % tile]
    codes_d, plane_d = T.wcd[:].bitcast(dt.uint8), T.wsd[:]
    codes_s, plane_s = T.wq[:, lo:hi].bitcast(dt.uint8), T.wp[:, lo:hi]

    if rank is None:
        g.wait_ge(T.sem.hs, bits(h_plane))
        write(dsts, plane_d, plane_s, arr, out)
        g.wait_ge(T.sem.hc, bits(h_codes))
        write(dsts, codes_d, codes_s, arr, out)
        g.wait_ge(T.sem.sent, sent[0])
        return

    g.scalar.dma_start(plane_d, T.ws[:]).then_inc(T.sem.ls, 16)
    g.sync.dma_start(codes_d, T.wc[:]).then_inc(T.sem.lc, 16)
    g.sync.dma_start(T.xb[:], T.x[:]).then_inc(T.sem.lx, 16)
    g.scalar.dma_start(plane_s, T.ws[:]).then_inc(T.sem.lo, 16)
    g.scalar.dma_start(codes_s, T.wc[:]).then_inc(T.sem.lo, 16)

    g.wait_ge(T.sem.ls, 16)
    write(hand[core], plane_d, plane_d, T.sem.hs, h_plane)
    g.wait_ge(T.sem.lc, 16)
    write(hand[core], codes_d, codes_d, T.sem.hc, h_codes)
    write(dsts, plane_d, plane_s, arr, out)
    write(dsts, codes_d, codes_s, arr, out)

    g.vector.wait_ge(T.sem.lx, 16)
    g.vector.quantize_mx(T.xq[:], T.xs[:], T.xb[:]).then_inc(T.sem.qx, 1)
    sender = {}
    for c, (j, l) in jobs.items():
        for t in l:
            sender[(j, t)] = c
    order = [rank] + sorted((j for j in range(N) if j != rank), key=lambda j: (due[(j, core)], j))
    g.tensor.wait_ge(T.sem.qx, 1)
    g.tensor.wait_ge(T.sem.lo, 32)
    for k, j in enumerate(order):
        w, wpl = T.wq[:, j * WW:(j + 1) * WW], T.wp[:, j * WW:(j + 1) * WW]
        blk = T.yb[:, j * NC:(j + 1) * NC]
        mm, cp = T.sem["mm%d" % k], T.sem["cp%d" % k]
        if j != rank:
            c = sender[(j, core)]
            g.tensor.wait_ge(T.sem["arr%d" % j], 2 * bits(engines(c, jobs[c][1], topo)))
        if k >= BANKS:
            g.tensor.wait_ge(T.sem["cp%d" % (k - BANKS)], 1)
        b0 = (k % BANKS) * BANK
        if k == N - 1:
            h = NC // 2
            b1 = ((k + 1) % BANKS) * BANK
            g.tensor.wait_ge(T.sem["cp%d" % (k + 1 - BANKS)], 1)
            g.tensor.matmul_mx(T.ps[:, b0:b0 + h], w, wpl, T.xq[:, 0:h], T.xs[:, 0:h], True, True).then_inc(mm, 1)
            g.tensor.matmul_mx(T.ps[:, b1:b1 + h], w, wpl, T.xq[:, h:NC], T.xs[:, h:NC], True, True).then_inc(T.sem.mmx, 1)
            g.vector.wait_ge(mm, 1)
            g.vector.tensor_copy(T.yb[:, j * NC:j * NC + h], T.ps[:, b0:b0 + h]).then_inc(cp, 1)
            g.vector.wait_ge(T.sem.mmx, 1)
            g.vector.tensor_copy(T.yb[:, j * NC + h:(j + 1) * NC], T.ps[:, b1:b1 + h]).then_inc(cp, 1)
            g.sync.wait_ge(cp, 2)
            g.sync.dma_start(T.y[:, j * NC:(j + 1) * NC], blk).then_inc(T.sem.st, 16)
            continue
        bank = T.ps[:, b0:b0 + NC]
        g.tensor.matmul_mx(bank, w, wpl, T.xq[:], T.xs[:], True, True).then_inc(mm, 1)
        if (N - 1 - k) % 2 == 0:
            g.vector.wait_ge(mm, 1)
            g.vector.tensor_copy(blk, bank).then_inc(cp, 1)
            q = g.sync
        else:
            g.scalar.wait_ge(mm, 1)
            g.scalar.activation(blk, bank, ActivationFunctionType.Copy).then_inc(cp, 1)
            q = g.scalar
        q.wait_ge(cp, 1)
        q.dma_start(T.y[:, j * NC:(j + 1) * NC], blk).then_inc(T.sem.st, 16)

    g.wait_ge(T.sem.sent, sent[0])
    g.wait_ge(T.sem.st, 16 * N)
